import numpy as np
import ml_dtypes

BF16 = ml_dtypes.bfloat16


def bf(x):
    return np.asarray(x, np.float32).astype(BF16)


def f32(x):
    return np.asarray(x, np.float32)


def f64(x):
    return np.asarray(x).astype(np.float64)


def striped(idx):
    return np.tile(idx.reshape(-1, 16).T, (8, 1))


def rows(idx, k):
    return np.tile(idx, (k, 1))


def look(tab, idx):
    return np.take_along_axis(f64(tab), rows(idx, len(tab)), axis=1)


K, S, V, N = 256, 2048, 1536, 1536


def setup_inputs():
    return {"tab": f32(np.random.standard_normal((2, K, S))), "x0": f32(np.random.standard_normal((K, V))), "offs": striped(np.random.randint(0, S, N))}


def reference(tab, x0, offs):
    idx = offs[:16].T.reshape(-1)
    x = f64(x0) * look(tab[0], idx) + look(tab[1], idx)
    return x

@@ -1,0 +1,49 @@
+import concourse.mybir as mybir
+
+F32 = mybir.dt.float32
+U16 = mybir.dt.uint16
+MULT = mybir.AluOpType.mult
+ADD = mybir.AluOpType.add
+
+ROWS = 128
+ENTRIES_PER_COLUMN = 16
+PIECE = 512
+
+
+def tile_lookup_film_mul_out_kernel(tc, tab, x0, offs, out):
+    nc = tc.nc
+    blocks = x0.shape[0] // ROWS
+    columns = x0.shape[1]
+    table_columns = tab.shape[2]
+
+    with tc.tile_pool(name="held", bufs=1) as held:
+        offsets = held.tile([ROWS, columns // ENTRIES_PER_COLUMN], U16, name="offsets")
+        nc.sync.dma_start(offsets[:], offs)
+
+        gains, shifts, features = [], [], []
+        for b in range(blocks):
+            rows = slice(b * ROWS, (b + 1) * ROWS)
+            gains.append(held.tile([ROWS, table_columns], F32, name=f"gains{b}"))
+            shifts.append(held.tile([ROWS, table_columns], F32, name=f"shifts{b}"))
+            features.append(held.tile([ROWS, columns], F32, name=f"features{b}"))
+            nc.sync.dma_start(gains[b][:], tab[0, rows, :])
+            nc.sync.dma_start(features[b][:], x0[rows, :])
+            nc.sync.dma_start(shifts[b][:], tab[1, rows, :])
+
+        for b in range(blocks):
+            rows = slice(b * ROWS, (b + 1) * ROWS)
+            product = held.tile([ROWS, columns], F32, name=f"product{b}")
+            result = held.tile([ROWS, columns], F32, name=f"result{b}")
+
+            for start in range(0, columns, PIECE):
+                piece = slice(start, start + PIECE)
+                entries = slice(start // ENTRIES_PER_COLUMN, (start + PIECE) // ENTRIES_PER_COLUMN)
+                looked_up = gains[b][:].indirect(offsets[:, entries])
+                nc.vector.tensor_tensor(product[:, piece], looked_up, features[b][:, piece], MULT)
+
+            for start in range(0, columns, PIECE):
+                piece = slice(start, start + PIECE)
+                entries = slice(start // ENTRIES_PER_COLUMN, (start + PIECE) // ENTRIES_PER_COLUMN)
+                looked_up = shifts[b][:].indirect(offsets[:, entries])
+                nc.vector.tensor_tensor(result[:, piece], looked_up, product[:, piece], ADD)
+                nc.scalar.dma_start(out[rows, piece], result[:, piece])

@@ -7,7 +7,18 @@ ADD = mybir.AluOpType.add
 
 ROWS = 128
 ENTRIES_PER_COLUMN = 16
-PIECE = 512
+
+GROWING = (256, 512, 768)
+SHRINKING = (768, 512, 256)
+
+
+def pieces(widths):
+    cuts, start = [], 0
+    for width in widths:
+        stop = start + width
+        cuts.append((slice(start, stop), slice(start // ENTRIES_PER_COLUMN, stop // ENTRIES_PER_COLUMN)))
+        start = stop
+    return cuts
 
 
 def tile_lookup_film_mul_out_kernel(tc, tab, x0, offs, out):
@@ -15,6 +26,8 @@ def tile_lookup_film_mul_out_kernel(tc, tab, x0, offs, out):
     blocks = x0.shape[0] // ROWS
     columns = x0.shape[1]
     table_columns = tab.shape[2]
+    product_pieces = [pieces(GROWING if b == 0 else (columns,)) for b in range(blocks)]
+    sum_pieces = [pieces(SHRINKING if b == blocks - 1 else (columns,)) for b in range(blocks)]
 
     with tc.tile_pool(name="held", bufs=1) as held:
         offsets = held.tile([ROWS, columns // ENTRIES_PER_COLUMN], U16, name="offsets")
@@ -27,7 +40,8 @@ def tile_lookup_film_mul_out_kernel(tc, tab, x0, offs, out):
             shifts.append(held.tile([ROWS, table_columns], F32, name=f"shifts{b}"))
             features.append(held.tile([ROWS, columns], F32, name=f"features{b}"))
             nc.sync.dma_start(gains[b][:], tab[0, rows, :])
-            nc.sync.dma_start(features[b][:], x0[rows, :])
+            for piece, entries in product_pieces[b]:
+                nc.sync.dma_start(features[b][:, piece], x0[rows, piece])
             nc.sync.dma_start(shifts[b][:], tab[1, rows, :])
 
         for b in range(blocks):
@@ -35,15 +49,11 @@ def tile_lookup_film_mul_out_kernel(tc, tab, x0, offs, out):
             product = held.tile([ROWS, columns], F32, name=f"product{b}")
             result = held.tile([ROWS, columns], F32, name=f"result{b}")
 
-            for start in range(0, columns, PIECE):
-                piece = slice(start, start + PIECE)
-                entries = slice(start // ENTRIES_PER_COLUMN, (start + PIECE) // ENTRIES_PER_COLUMN)
+            for piece, entries in product_pieces[b]:
                 looked_up = gains[b][:].indirect(offsets[:, entries])
                 nc.vector.tensor_tensor(product[:, piece], looked_up, features[b][:, piece], MULT)
 
-            for start in range(0, columns, PIECE):
-                piece = slice(start, start + PIECE)
-                entries = slice(start // ENTRIES_PER_COLUMN, (start + PIECE) // ENTRIES_PER_COLUMN)
+            for piece, entries in sum_pieces[b]:
                 looked_up = shifts[b][:].indirect(offsets[:, entries])
                 nc.vector.tensor_tensor(result[:, piece], looked_up, product[:, piece], ADD)
                 nc.scalar.dma_start(out[rows, piece], result[:, piece])

@@ -26,8 +26,8 @@ def tile_lookup_film_mul_out_kernel(tc, tab, x0, offs, out):
     blocks = x0.shape[0] // ROWS
     columns = x0.shape[1]
     table_columns = tab.shape[2]
-    product_pieces = [pieces(GROWING if b == 0 else (columns,)) for b in range(blocks)]
-    sum_pieces = [pieces(SHRINKING if b == blocks - 1 else (columns,)) for b in range(blocks)]
+    product_pieces = pieces(GROWING)
+    sum_pieces = pieces(SHRINKING)
 
     with tc.tile_pool(name="held", bufs=1) as held:
         offsets = held.tile([ROWS, columns // ENTRIES_PER_COLUMN], U16, name="offsets")
@@ -40,7 +40,7 @@ def tile_lookup_film_mul_out_kernel(tc, tab, x0, offs, out):
             shifts.append(held.tile([ROWS, table_columns], F32, name=f"shifts{b}"))
             features.append(held.tile([ROWS, columns], F32, name=f"features{b}"))
             nc.sync.dma_start(gains[b][:], tab[0, rows, :])
-            for piece, entries in product_pieces[b]:
+            for piece, entries in product_pieces:
                 nc.sync.dma_start(features[b][:, piece], x0[rows, piece])
             nc.sync.dma_start(shifts[b][:], tab[1, rows, :])
 
@@ -49,11 +49,11 @@ def tile_lookup_film_mul_out_kernel(tc, tab, x0, offs, out):
             product = held.tile([ROWS, columns], F32, name=f"product{b}")
             result = held.tile([ROWS, columns], F32, name=f"result{b}")
 
-            for piece, entries in product_pieces[b]:
+            for piece, entries in product_pieces:
                 looked_up = gains[b][:].indirect(offsets[:, entries])
                 nc.vector.tensor_tensor(product[:, piece], looked_up, features[b][:, piece], MULT)
 
-            for piece, entries in sum_pieces[b]:
+            for piece, entries in sum_pieces:
                 looked_up = shifts[b][:].indirect(offsets[:, entries])
                 nc.vector.tensor_tensor(result[:, piece], looked_up, product[:, piece], ADD)
                 nc.scalar.dma_start(out[rows, piece], result[:, piece])

import concourse.mybir as mybir

F32 = mybir.dt.float32
U16 = mybir.dt.uint16
MULT = mybir.AluOpType.mult
ADD = mybir.AluOpType.add

ROWS = 128
ENTRIES_PER_COLUMN = 16

GROWING = (256, 512, 768)
SHRINKING = (768, 512, 256)


def pieces(widths):
    cuts, start = [], 0
    for width in widths:
        stop = start + width
        cuts.append((slice(start, stop), slice(start // ENTRIES_PER_COLUMN, stop // ENTRIES_PER_COLUMN)))
        start = stop
    return cuts


def tile_lookup_film_mul_out_kernel(tc, tab, x0, offs, out):
    nc = tc.nc
    blocks = x0.shape[0] // ROWS
    columns = x0.shape[1]
    table_columns = tab.shape[2]
    product_pieces = pieces(GROWING)
    sum_pieces = pieces(SHRINKING)

    with tc.tile_pool(name="held", bufs=1) as held:
        offsets = held.tile([ROWS, columns // ENTRIES_PER_COLUMN], U16, name="offsets")
        nc.sync.dma_start(offsets[:], offs)

        gains, shifts, features = [], [], []
        for b in range(blocks):
            rows = slice(b * ROWS, (b + 1) * ROWS)
            gains.append(held.tile([ROWS, table_columns], F32, name=f"gains{b}"))
            shifts.append(held.tile([ROWS, table_columns], F32, name=f"shifts{b}"))
            features.append(held.tile([ROWS, columns], F32, name=f"features{b}"))
            nc.sync.dma_start(gains[b][:], tab[0, rows, :])
            for piece, entries in product_pieces:
                nc.sync.dma_start(features[b][:, piece], x0[rows, piece])
            nc.sync.dma_start(shifts[b][:], tab[1, rows, :])

        for b in range(blocks):
            rows = slice(b * ROWS, (b + 1) * ROWS)
            product = held.tile([ROWS, columns], F32, name=f"product{b}")
            result = held.tile([ROWS, columns], F32, name=f"result{b}")

            for piece, entries in product_pieces:
                looked_up = gains[b][:].indirect(offsets[:, entries])
                nc.vector.tensor_tensor(product[:, piece], looked_up, features[b][:, piece], MULT)

            for piece, entries in sum_pieces:
                looked_up = shifts[b][:].indirect(offsets[:, entries])
                nc.vector.tensor_tensor(result[:, piece], looked_up, product[:, piece], ADD)
                nc.scalar.dma_start(out[rows, piece], result[:, piece])
